import numpy as np
import ml_dtypes


def mxq(x, axis, fmt="e4m3"):
    dtype, down = {"e4m3": (ml_dtypes.float8_e4m3fn, 7), "e5m2": (ml_dtypes.float8_e5m2, 14)}[fmt]
    v = np.moveaxis(np.asarray(x, np.float32).astype(ml_dtypes.bfloat16).astype(np.float64), axis, -1)
    blocks = v.reshape(v.shape[:-1] + (-1, 32))
    amax = np.abs(blocks).max(-1, keepdims=True)
    byte = np.maximum(np.where(amax > 0, np.frexp(amax)[1] - 1 + 127, 0) - down, 1)
    scale = np.exp2(byte - 127.0)
    codes = (blocks / scale).astype(np.float32).astype(dtype).astype(np.float64)
    return np.moveaxis((codes * scale).reshape(v.shape), -1, axis)


WIDE = False


def mx_kscale(k):
    if not WIDE:
        return np.ones(k)
    levels = np.array([10, -10, 5, -5, 0])
    if k % 512:
        return np.exp2(np.random.permutation(np.resize(levels, k // 32))).repeat(32)
    a = np.empty((k // 512, 16))
    for p in range(k // 512):
        a[p, :8] = np.random.permutation(np.resize(levels, 8))
        for g in range(8):
            far = levels[np.abs(levels - a[p, g]) >= 10]
            a[p, g + 8] = far[np.random.randint(len(far))]
    return np.exp2(a.ravel()).repeat(32)


def f64(x):
    return np.asarray(x).astype(np.float64)


def striped(idx):
    return np.tile(idx.reshape(-1, 16).T, (8, 1)).astype(np.uint16)


def unstriped(offs):
    return offs[:16].T.reshape(-1).astype(np.int64)


E2M1 = np.array([0.0, 0.5, 1.0, 1.5, 2.0, 3.0, 4.0, 6.0, -0.0, -0.5, -1.0, -1.5, -2.0, -3.0, -4.0, -6.0])


def pack_weight(w, fmt):
    k, n = w.shape
    w = f64(np.asarray(w, np.float32).astype(ml_dtypes.bfloat16)).reshape(k // 32, 32, n)
    amax = np.abs(w).max(1)
    if fmt == "e4m3":
        byte = np.frexp(amax)[1] - 1 + 127 - 7
    else:
        mant, ex = np.frexp(amax / 6.0)
        byte = np.where(mant > 0.5, ex, ex - 1) + 127
    byte = np.clip(np.where(amax > 0, byte, 1), 1, 254)
    scaled = (w * np.exp2(127.0 - byte)[:, None, :]).reshape(k, n).astype(np.float32)
    by_word = np.ascontiguousarray(scaled.reshape(k // 512, 128, 4, n).transpose(0, 1, 3, 2))
    if fmt == "e4m3":
        words = by_word.astype(ml_dtypes.float8_e4m3fn).view(np.uint8)
    else:
        c = by_word.astype(ml_dtypes.float4_e2m1fn).view(np.uint8) & 0xF
        words = (c[..., 0::2] | (c[..., 1::2] << 4)).reshape(k // 512, 128, 2 * n)
    return np.ascontiguousarray(words), np.ascontiguousarray(byte.astype(np.uint8).reshape(k // 512, 16, n))


def unpack_weight(words, scales, fmt):
    g, _, n = scales.shape
    words = np.ascontiguousarray(words).reshape(g, 128, n, -1)
    if fmt == "e4m3":
        vals = words.view(ml_dtypes.float8_e4m3fn).astype(np.float64)
    else:
        nib = np.empty((g, 128, n, 4), np.uint8)
        nib[..., 0::2] = words & 0xF
        nib[..., 1::2] = words >> 4
        vals = E2M1[nib]
    vals = vals * np.repeat(np.exp2(scales.astype(np.float64) - 127.0), 8, axis=1)[..., None]
    return vals.transpose(0, 1, 3, 2).reshape(g * 512, n)


def gelu(v):
    return 0.5 * v * (1.0 + np.tanh(np.sqrt(2.0 / np.pi) * (v + 0.044715 * v**3)))


def twice(P):
    return np.random.permutation(np.repeat(np.arange(P), 2))


K, H, T, S, P = 1024, 1024, 4096, 1024, 512

def setup_inputs():
    n = np.random.standard_normal
    s = mx_kscale(K)[:, None]
    u = mx_kscale(H)[:, None]
    d = {}
    d["tab_words"], d["tab_scales"] = pack_weight(n((K, T)) * s, "e4m3")
    d["offs"] = striped(np.random.permutation(T)[:S])
    d["pos1"] = striped(np.random.permutation(S)[:P])
    d["pos2"] = striped(np.random.permutation(S)[:P])
    d["pos3"] = striped(twice(P))
    d["w1"] = (n((K, H)) / K ** 0.5 / s * u.T).astype(np.float32)
    d["b1"] = (0.5 * n(H) * u[:, 0]).astype(np.float32)
    d["gv"] = np.exp(0.4 * n(H)).astype(np.float32)
    d["w4_words"], d["w4_scales"] = pack_weight(n((H, H)) / H ** 0.5 / u, "e2m1")
    d["b2"] = (0.5 * n(H)).astype(np.float32)
    d["sc"] = (np.exp(0.3 * n(H)) / u[:, 0]).astype(np.float32)
    return d

def reference(tab_words, tab_scales, offs, pos1, pos2, pos3, w1, b1, gv, w4_words, w4_scales, b2, sc):
    v = unpack_weight(tab_words, tab_scales, "e4m3")[:, unstriped(offs)]
    h = (mxq(f64(w1), 0, "e4m3").T @ v) + f64(b1)[:, None]
    top = h[:, unstriped(pos1)]
    bottom = f64(gv)[:, None] * h[:, unstriped(pos2)]
    z = np.maximum(top, bottom)
    w4 = unpack_weight(w4_words, w4_scales, "e2m1")
    y = (w4.T @ mxq(z, 0, "e4m3")) + f64(b2)[:, None]
    up = y[:, unstriped(pos3)]
    out = np.square(up) + f64(sc)[:, None] * h
    return out

@@ -1,0 +1,297 @@
+from contextlib import ExitStack
+
+import concourse.mybir as mybir
+
+K, H, T, S, M = 1024, 1024, 4096, 1024, 512
+FLOPS = 2 * K * H * S + 2 * H * H * M
+
+F32 = mybir.dt.float32
+BF16 = mybir.dt.bfloat16
+I32 = mybir.dt.int32
+U32 = mybir.dt.uint32
+U16 = mybir.dt.uint16
+U8 = mybir.dt.uint8
+E4M3 = mybir.dt.float8_e4m3fn_x4
+E2M1 = mybir.dt.float4_e2m1fn_x4
+ALU = mybir.AluOpType
+ACT = mybir.ActivationFunctionType
+
+P = 128
+PACK = 4
+KP = P * PACK
+BANK = 512
+TILES = H // P
+SLOT = S + M
+Y_WIN = S + 32
+SC_AHEAD = 3
+LAST_Z = [(0, 256), (256, 384), (384, 512)]
+LAST_OUT = [(0, 512), (512, 768), (768, 1024)]
+
+
+def tile_list_stopper_leak_features_kernel(
+    tc, tab_words, tab_scales, offs, pos1, pos2, pos3, w1, b1, gv, w4_words, w4_scales, b2, sc, out
+):
+    nc = tc.nc
+    with ExitStack() as ctx:
+        keep = ctx.enter_context(tc.tile_pool(name="keep", bufs=1))
+        ring = ctx.enter_context(tc.tile_pool(name="ring", bufs=3))
+        psum = ctx.enter_context(tc.psum_pool(name="psum", bufs=8))
+
+        def held(shape, dtype, name):
+            return keep.tile(shape, dtype, name=name, align_bytes=64)
+
+        def load_list(src, name):
+            lst = keep.tile(list(src.shape), U16, name=name)
+            nc.sync.dma_start(lst[:], src)
+            return lst
+
+        def load_table(a):
+            words = held([P, T], U32, "tab_w%d" % a)
+            nc.sync.dma_start(words[:].bitcast(I32), tab_words[a].rearrange("p t i -> p (t i)").bitcast(I32))
+            return words
+
+        hz = held([P, (TILES + 1) * SLOT], F32, "hz")
+
+        def load_w1(raw, a, c0, c1):
+            raw = raw.rearrange("p (j c) -> p j c", j=PACK)
+            nc.sync.dma_start(raw, w1[a * KP : (a + 1) * KP, c0:c1].rearrange("(p j) c -> p j c", j=PACK))
+            return raw
+
+        def load_vector(src, name):
+            vec = held([P, TILES], F32, name)
+            nc.sync.dma_start(
+                vec[:].rearrange("p (b t) -> p b t", t=PACK), src.rearrange("(b p t) -> p b t", p=P, t=PACK)
+            )
+            return vec
+
+        tab_s = held([P, T], U8, "tab_s")
+        nc.vector.memset(tab_s[0:96, :].bitcast(I32), 0)
+        v_s = held([P, S], U8, "v_s")
+        nc.vector.memset(v_s[:].bitcast(I32), 0)
+        w4_s = held([P, 2 * H], U8, "w4_s")
+        nc.vector.memset(w4_s[:].bitcast(I32), 0)
+
+        offs_t = load_list(offs, "offs_t")
+        nc.sync.dma_start(tab_s[96:P, :].bitcast(I32), tab_scales.rearrange("a q t -> (a q) t").bitcast(I32))
+        tab_w0 = load_table(0)
+        raw00 = load_w1(held([P, PACK * 512], F32, "raw00")[:], 0, 0, 512)
+        tab_w1 = load_table(1)
+        raw10 = [load_w1(held([P, PACK * 256], F32, "raw10_%d" % c0)[:], 1, c0, c0 + 256) for c0 in (0, 256)]
+        pos1_t = load_list(pos1, "pos1_t")
+        pos2_t = load_list(pos2, "pos2_t")
+        b1_t = load_vector(b1, "b1_t")
+        gv_t = load_vector(gv, "gv_t")
+        for q in range(4):
+            nc.sync.dma_start(
+                w4_s[32 * q : 32 * q + 4, :].bitcast(I32).rearrange("r (a n) -> r a n", a=2),
+                w4_scales[:, 4 * q : 4 * q + 4, :].bitcast(I32).rearrange("a r n -> r a n"),
+            )
+        w4_w = held([P, 2 * H], U16, "w4_w")
+        nc.sync.dma_start(
+            w4_w[:].bitcast(I32).rearrange("p (a n) -> p a n", a=2),
+            w4_words.bitcast(I32).rearrange("a p n -> p a n"),
+        )
+        raw01 = load_w1(hz[:, SLOT + S : 3 * SLOT], 0, 512, 1024)
+        raw11 = load_w1(hz[:, 3 * SLOT : 3 * SLOT + PACK * 512], 1, 512, 1024)
+        sc_t = load_vector(sc, "sc_t")
+        b2_t = load_vector(b2, "b2_t")
+        pos3_t = load_list(pos3, "pos3_t")
+
+        v_w = [held([P, S], U32, "v_w%d" % a) for a in range(2)]
+        v_rows = held([P, S], U8, "v_rows")
+        w1_w = [[held([P, KP], U32, "w1_w%d%d" % (a, b)) for b in range(2)] for a in range(2)]
+        w1_s = [[held([P, KP], U8, "w1_s%d%d" % (a, b)) for b in range(2)] for a in range(2)]
+
+        def gather_table(words, a):
+            for s in range(2):
+                nc.vector.tensor_copy(
+                    v_w[a][:, s * BANK : (s + 1) * BANK], words[:].indirect(offs_t[:, s * 32 : (s + 1) * 32])
+                )
+
+        def deal_views(grouped, raw, m0):
+            width = raw.shape[2] // PACK
+            dst = grouped[:].rearrange("p (t m j) -> p m j t", t=PACK, j=PACK)[:, m0 : m0 + width]
+            return dst, raw.rearrange("p j (m t) -> p m j t", t=PACK)
+
+        def cast_w1(grouped, raw, m0=0):
+            dst, src = deal_views(grouped, raw, m0)
+            nc.scalar.activation(dst, src, ACT.Copy)
+
+        def quantise(words, scales, grouped, c0, c1):
+            nc.vector.quantize_mx(
+                out=words[:, c0:c1].bitcast(E4M3), scales=scales[:, c0:c1], in_=grouped[:, PACK * c0 : PACK * c1]
+            )
+
+        def h_pass(bank, a, c, s):
+            b, t = divmod(c, PACK)
+            cols = slice(t * P, (t + 1) * P)
+            picks = slice(s * BANK, (s + 1) * BANK)
+            nc.tensor.matmul_mx(
+                out=bank[:],
+                lhsT=w1_w[a][b][:, cols].bitcast(E4M3),
+                lhsT_scale=w1_s[a][b][:, cols],
+                rhs=v_w[a][:, picks].bitcast(E4M3),
+                rhs_scale=v_s[4 * a : P, picks],
+                start=(a == 0),
+                stop=(a == 1),
+            )
+
+        z_planes = hz[:].rearrange("p (s x) -> p s x", x=SLOT)
+
+        def h_rows(c, width=S):
+            return hz[:, c * SLOT : c * SLOT + width]
+
+        def empty_h(banks, c):
+            for s in range(2):
+                nc.scalar.activation(
+                    h_rows(c)[:, s * BANK : (s + 1) * BANK], banks[s][:], ACT.Identity, bias=b1_t[:, c : c + 1]
+                )
+
+        def new_banks(c):
+            return [psum.tile([P, BANK], F32, name="h_bank%d_%d" % (c, s), tag="bank") for s in range(2)]
+
+        nc.vector.tensor_copy(v_rows[:], tab_s[:].indirect(offs_t[:]))
+        for a in range(2):
+            for q in range(4):
+                row = 96 + 16 * a + 4 * q
+                nc.gpsimd.dma_start(
+                    v_s[32 * q + 4 * a : 32 * q + 4 * a + 4, :].bitcast(I32), v_rows[row : row + 4, :].bitcast(I32)
+                )
+        gather_table(tab_w0, 0)
+        g00 = keep.tile([P, PACK * KP], BF16, name="g00", tag="g00", align_bytes=64)
+        cast_w1(g00, raw00)
+        quantise(w1_w[0][0], w1_s[0][0], g00, 0, KP)
+        w4_sp = keep.tile([P, 2 * H], U8, name="w4_sp", tag="g00", align_bytes=64)
+        nc.vector.tensor_copy(
+            w4_sp[:].rearrange("p (g t m) -> p g t m", t=PACK, m=P),
+            w4_s[:].rearrange("p (g m t) -> p g t m", t=PACK, m=P),
+        )
+        gather_table(tab_w1, 1)
+        g10 = held([P, PACK * KP], BF16, "g10")
+        cast_w1(g10, raw10[0])
+        dst, src = deal_views(g10, raw10[1], 64)
+        nc.vector.tensor_copy(dst, src)
+        for t in range(PACK):
+            quantise(w1_w[1][0], w1_s[1][0], g10, t * P, (t + 1) * P)
+        w4_wp = held([P, 2 * H], U16, "w4_wp")
+        nc.vector.tensor_copy(
+            w4_wp[:].rearrange("p (g t m) -> p g t m", t=PACK, m=P),
+            w4_w[:].rearrange("p (g m t) -> p g t m", t=PACK, m=P),
+        )
+
+        banks = [new_banks(c) for c in range(PACK)]
+        for c in range(PACK):
+            for a in range(2):
+                for s in range(2):
+                    h_pass(banks[c][s], a, c, s)
+
+        g01 = held([P, PACK * KP], BF16, "g01")
+        g11 = held([P, PACK * KP], BF16, "g11")
+        for c in range(2):
+            empty_h(banks[c], c)
+        cast_w1(g01, raw01)
+        empty_h(banks[2], 2)
+        cast_w1(g11, raw11)
+        empty_h(banks[3], 3)
+
+        def pick(c, m0, m1, width):
+            top = ring.tile([P, m1 - m0], F32, name="top", tag="top")
+            bottom = ring.tile([P, m1 - m0], F32, name="bottom", tag="bottom")
+            cols = slice(m0 // 16, m1 // 16)
+            nc.vector.tensor_copy(top[:], h_rows(c, width).indirect(pos1_t[:, cols]))
+            nc.vector.tensor_copy(bottom[:], h_rows(c).indirect(pos2_t[:, cols]))
+            return c, m0, m1, top, bottom
+
+        def join(c, m0, m1, top, bottom):
+            nc.vector.scalar_tensor_tensor(
+                out=hz[:, (c + 1) * SLOT + S + m0 : (c + 1) * SLOT + S + m1],
+                in0=bottom[:],
+                scalar=gv_t[:, c : c + 1],
+                in1=top[:],
+                op0=ALU.mult,
+                op1=ALU.max,
+            )
+
+        z_g = [held([P, PACK * M], BF16, "z_g%d" % b) for b in range(2)]
+        z_w = [held([P, M], U32, "z_w%d" % b) for b in range(2)]
+        z_s = [held([P, M], U8, "z_s%d" % b) for b in range(2)]
+
+        def weave(b, m0, m1):
+            planes = z_planes[:, PACK * b + 1 : PACK * b + 1 + PACK, S + m0 : S + m1]
+            nc.scalar.copy(
+                z_g[b][:, PACK * m0 : PACK * m1].rearrange("p (c i t) -> p c t i", i=4, t=PACK),
+                planes.rearrange("p t (c i) -> p c t i", i=4),
+            )
+
+        scaled = {}
+        out_order = [(c + PACK) % TILES for c in range(TILES)]
+
+        def scale_h(c):
+            scaled[c] = ring.tile([P, S], F32, name="scaled", tag="scaled")
+            nc.scalar.activation(scaled[c][:], h_rows(c), ACT.Copy, scale=sc_t[:, c : c + 1])
+
+        picked = pick(0, 0, M, S)
+        for c in range(1, PACK):
+            ahead = pick(c, 0, M, SLOT)
+            join(*picked)
+            picked = ahead
+            if c == 1:
+                quantise(w1_w[0][1], w1_s[0][1], g01, 0, KP)
+            if c == 2:
+                quantise(w1_w[1][1], w1_s[1][1], g11, 0, KP)
+        for c in range(PACK, TILES):
+            banks = new_banks(c)
+            for a in range(2):
+                for s in range(2):
+                    h_pass(banks[s], a, c, s)
+            empty_h(banks, c)
+        for c in range(PACK, TILES - 1):
+            ahead = pick(c, 0, M, SLOT)
+            join(*picked)
+            picked = ahead
+            if c == PACK:
+                weave(0, 0, M)
+                for first in out_order[:SC_AHEAD]:
+                    scale_h(first)
+        quantise(z_w[0], z_s[0], z_g[0], 0, M)
+        for m0, m1 in LAST_Z:
+            ahead = pick(TILES - 1, m0, m1, SLOT if m0 == 0 else S)
+            join(*picked)
+            picked = ahead
+        join(*picked)
+        for m0, m1 in LAST_Z:
+            weave(1, m0, m1)
+            quantise(z_w[1], z_s[1], z_g[1], m0, m1)
+
+        def y_pass(bank, a, c, m0, m1, stop):
+            cols = slice(a * H + c * P, a * H + (c + 1) * P)
+            nc.tensor.matmul_mx(
+                out=bank[:, m0:m1],
+                lhsT=w4_wp[:, cols].bitcast(E2M1),
+                lhsT_scale=w4_sp[:, cols],
+                rhs=z_w[a][:, m0:m1].bitcast(E4M3),
+                rhs_scale=z_s[a][:, m0:m1],
+                start=(a == 0),
+                stop=stop,
+            )
+
+        out_rows = out.rearrange("(b p t) j -> b t p j", p=P, t=PACK)
+        for i, c in enumerate(out_order):
+            bank = psum.tile([P, BANK], F32, name="y_bank%d" % c, tag="bank")
+            y_pass(bank, 0, c, 0, M, False)
+            step = P if i == 0 else M
+            for m0 in range(0, M, step):
+                y_pass(bank, 1, c, m0, m0 + step, m0 + step == M)
+            squares = ring.tile([P, Y_WIN], F32, name="squares", tag="squares")
+            nc.scalar.activation(squares[:, 0:M], bank[:], ACT.Square, bias=b2_t[:, c : c + 1])
+            if i >= SC_AHEAD:
+                scale_h(c)
+            result = ring.tile([P, S], F32, name="result", tag="result")
+            for j0, j1 in LAST_OUT if i == TILES - 1 else [(0, S)]:
+                nc.vector.tensor_tensor(
+                    result[:, j0:j1],
+                    squares[:].indirect(pos3_t[:, j0 // 16 : j1 // 16]),
+                    scaled[c][:, j0:j1],
+                    ALU.add,
+                )
+                nc.sync.dma_start(out_rows[c // PACK, c % PACK, :, j0:j1], result[:, j0:j1])

@@ -25,7 +25,7 @@ SLOT = S + M
 Y_WIN = S + 32
 SC_AHEAD = 3
 LAST_Z = [(0, 256), (256, 384), (384, 512)]
-LAST_OUT = [(0, 512), (512, 768), (768, 1024)]
+LAST_OUT = [(0, 512), (512, 896), (896, 1024)]
 
 
 def tile_list_stopper_leak_features_kernel(
@@ -64,15 +64,19 @@ def tile_list_stopper_leak_features_kernel(
             )
             return vec
 
-        tab_s = held([P, T], U8, "tab_s")
-        nc.vector.memset(tab_s[0:96, :].bitcast(I32), 0)
-        v_s = held([P, S], U8, "v_s")
-        nc.vector.memset(v_s[:].bitcast(I32), 0)
-        w4_s = held([P, 2 * H], U8, "w4_s")
-        nc.vector.memset(w4_s[:].bitcast(I32), 0)
+        tab_s = keep.tile([P, T], U8, name="tab_s", tag="tab_s", align_bytes=64)
+        nc.vector.memset(tab_s[:].bitcast(I32), 0)
+        for q in range(4):
+            nc.gpsimd.dma_start(
+                tab_s[32 * q : 32 * q + 8, :].bitcast(I32), tab_scales[:, 4 * q : 4 * q + 4, :].bitcast(I32)
+            )
+        w4_s = held([P, H], U8, "w4_s")
+        nc.vector.memset(w4_s[0:96, :].bitcast(I32), 0)
+        w4_sp = held([P, 2 * H], U8, "w4_sp")
+        nc.vector.memset(w4_sp[:].bitcast(I32), 0)
 
         offs_t = load_list(offs, "offs_t")
-        nc.sync.dma_start(tab_s[96:P, :].bitcast(I32), tab_scales.rearrange("a q t -> (a q) t").bitcast(I32))
+        nc.sync.dma_start(w4_s[96:P, :].bitcast(I32), w4_scales.rearrange("a q n -> (a q) n").bitcast(I32))
         tab_w0 = load_table(0)
         raw00 = load_w1(held([P, PACK * 512], F32, "raw00")[:], 0, 0, 512)
         tab_w1 = load_table(1)
@@ -81,11 +85,6 @@ def tile_list_stopper_leak_features_kernel(
         pos2_t = load_list(pos2, "pos2_t")
         b1_t = load_vector(b1, "b1_t")
         gv_t = load_vector(gv, "gv_t")
-        for q in range(4):
-            nc.sync.dma_start(
-                w4_s[32 * q : 32 * q + 4, :].bitcast(I32).rearrange("r (a n) -> r a n", a=2),
-                w4_scales[:, 4 * q : 4 * q + 4, :].bitcast(I32).rearrange("a r n -> r a n"),
-            )
         w4_w = held([P, 2 * H], U16, "w4_w")
         nc.sync.dma_start(
             w4_w[:].bitcast(I32).rearrange("p (a n) -> p a n", a=2),
@@ -97,8 +96,8 @@ def tile_list_stopper_leak_features_kernel(
         b2_t = load_vector(b2, "b2_t")
         pos3_t = load_list(pos3, "pos3_t")
 
-        v_w = [held([P, S], U32, "v_w%d" % a) for a in range(2)]
-        v_rows = held([P, S], U8, "v_rows")
+        v_w = [held([P, S], U32, "v_w0")]
+        v_s = held([P, S], U8, "v_s")
         w1_w = [[held([P, KP], U32, "w1_w%d%d" % (a, b)) for b in range(2)] for a in range(2)]
         w1_s = [[held([P, KP], U8, "w1_s%d%d" % (a, b)) for b in range(2)] for a in range(2)]
 
@@ -150,22 +149,23 @@ def tile_list_stopper_leak_features_kernel(
         def new_banks(c):
             return [psum.tile([P, BANK], F32, name="h_bank%d_%d" % (c, s), tag="bank") for s in range(2)]
 
-        nc.vector.tensor_copy(v_rows[:], tab_s[:].indirect(offs_t[:]))
+        w4_rows = held([P, H], U8, "w4_rows")
+        nc.vector.tensor_copy(
+            w4_rows[:].rearrange("p (g t m) -> p g t m", t=PACK, m=P),
+            w4_s[:].rearrange("p (g m t) -> p g t m", t=PACK, m=P),
+        )
         for a in range(2):
             for q in range(4):
                 row = 96 + 16 * a + 4 * q
-                nc.gpsimd.dma_start(
-                    v_s[32 * q + 4 * a : 32 * q + 4 * a + 4, :].bitcast(I32), v_rows[row : row + 4, :].bitcast(I32)
+                nc.sync.dma_start(
+                    w4_sp[32 * q : 32 * q + 4, a * H : (a + 1) * H].bitcast(I32), w4_rows[row : row + 4, :].bitcast(I32)
                 )
         gather_table(tab_w0, 0)
-        g00 = keep.tile([P, PACK * KP], BF16, name="g00", tag="g00", align_bytes=64)
+        nc.vector.tensor_copy(v_s[:], tab_s[:].indirect(offs_t[:]))
+        v_w.append(keep.tile([P, S], U32, name="v_w1", tag="tab_s", align_bytes=64))
+        g00 = held([P, PACK * KP], BF16, "g00")
         cast_w1(g00, raw00)
         quantise(w1_w[0][0], w1_s[0][0], g00, 0, KP)
-        w4_sp = keep.tile([P, 2 * H], U8, name="w4_sp", tag="g00", align_bytes=64)
-        nc.vector.tensor_copy(
-            w4_sp[:].rearrange("p (g t m) -> p g t m", t=PACK, m=P),
-            w4_s[:].rearrange("p (g m t) -> p g t m", t=PACK, m=P),
-        )
         gather_table(tab_w1, 1)
         g10 = held([P, PACK * KP], BF16, "g10")
         cast_w1(g10, raw10[0])
@@ -263,30 +263,33 @@ def tile_list_stopper_leak_features_kernel(
             weave(1, m0, m1)
             quantise(z_w[1], z_s[1], z_g[1], m0, m1)
 
-        def y_pass(bank, a, c, m0, m1, stop):
-            cols = slice(a * H + c * P, a * H + (c + 1) * P)
-            nc.tensor.matmul_mx(
-                out=bank[:, m0:m1],
-                lhsT=w4_wp[:, cols].bitcast(E2M1),
-                lhsT_scale=w4_sp[:, cols],
-                rhs=z_w[a][:, m0:m1].bitcast(E4M3),
-                rhs_scale=z_s[a][:, m0:m1],
-                start=(a == 0),
-                stop=stop,
-            )
+        def y_group(c, m0, m1, step, squares):
+            bank = psum.tile([P, m1 - m0], F32, name="y_bank", tag="bank")
+            for a in range(2):
+                cols = slice(a * H + c * P, a * H + (c + 1) * P)
+                for m in range(m0, m1, step):
+                    nc.tensor.matmul_mx(
+                        out=bank[:, m - m0 : m - m0 + step],
+                        lhsT=w4_wp[:, cols].bitcast(E2M1),
+                        lhsT_scale=w4_sp[:, cols],
+                        rhs=z_w[a][:, m : m + step].bitcast(E4M3),
+                        rhs_scale=z_s[a][:, m : m + step],
+                        start=(a == 0 and m == m0),
+                        stop=(a == 1 and m + step == m1),
+                    )
+            nc.scalar.activation(squares[:, m0:m1], bank[:], ACT.Square, bias=b2_t[:, c : c + 1])
 
         out_rows = out.rearrange("(b p t) j -> b t p j", p=P, t=PACK)
         for i, c in enumerate(out_order):
-            bank = psum.tile([P, BANK], F32, name="y_bank%d" % c, tag="bank")
-            y_pass(bank, 0, c, 0, M, False)
-            step = P if i == 0 else M
-            for m0 in range(0, M, step):
-                y_pass(bank, 1, c, m0, m0 + step, m0 + step == M)
             squares = ring.tile([P, Y_WIN], F32, name="squares", tag="squares")
-            nc.scalar.activation(squares[:, 0:M], bank[:], ACT.Square, bias=b2_t[:, c : c + 1])
+            if i == 0:
+                y_group(c, 0, M - P, P, squares)
+                y_group(c, M - P, M, P, squares)
+            else:
+                y_group(c, 0, M, M, squares)
             if i >= SC_AHEAD:
                 scale_h(c)
-            result = ring.tile([P, S], F32, name="result", tag="result")
+            result = ring.tile([P, S], F32, name="result", tag="result", bufs=4)
             for j0, j1 in LAST_OUT if i == TILES - 1 else [(0, S)]:
                 nc.vector.tensor_tensor(
                     result[:, j0:j1],

@@ -21,9 +21,10 @@ PACK = 4
 KP = P * PACK
 BANK = 512
 TILES = H // P
+PAIR = 2 * P
 SLOT = S + M
 Y_WIN = S + 32
-SC_AHEAD = 3
+SC_AHEAD = 2
 LAST_Z = [(0, 256), (256, 384), (384, 512)]
 LAST_OUT = [(0, 512), (512, 896), (896, 1024)]
 
@@ -38,7 +39,7 @@ def tile_list_stopper_leak_features_kernel(
         psum = ctx.enter_context(tc.psum_pool(name="psum", bufs=8))
 
         def held(shape, dtype, name):
-            return keep.tile(shape, dtype, name=name, align_bytes=64)
+            return keep.tile(shape, dtype, name=name, tag=name, align_bytes=64)
 
         def load_list(src, name):
             lst = keep.tile(list(src.shape), U16, name=name)
@@ -57,12 +58,16 @@ def tile_list_stopper_leak_features_kernel(
             nc.sync.dma_start(raw, w1[a * KP : (a + 1) * KP, c0:c1].rearrange("(p j) c -> p j c", j=PACK))
             return raw
 
-        def load_vector(src, name):
-            vec = held([P, TILES], F32, name)
-            nc.sync.dma_start(
-                vec[:].rearrange("p (b t) -> p b t", t=PACK), src.rearrange("(b p t) -> p b t", p=P, t=PACK)
-            )
-            return vec
+        def load_plain(src, name):
+            vec = held([P, PACK], F32, name)
+            with nc.allow_non_contiguous_dma(reason="one value a partition and tile"):
+                nc.sync.dma_start(vec[:], src[0:KP].rearrange("(c p) -> p c", p=P))
+            return [vec[:, c : c + 1] for c in range(PACK)]
+
+        def load_dealt(src, name):
+            vec = held([P, PACK], F32, name)
+            nc.sync.dma_start(vec[:], src[KP:H].rearrange("(p t) -> p t", t=PACK))
+            return [vec[:, t : t + 1] for t in range(PACK)]
 
         tab_s = keep.tile([P, T], U8, name="tab_s", tag="tab_s", align_bytes=64)
         nc.vector.memset(tab_s[:].bitcast(I32), 0)
@@ -75,84 +80,110 @@ def tile_list_stopper_leak_features_kernel(
         w4_sp = held([P, 2 * H], U8, "w4_sp")
         nc.vector.memset(w4_sp[:].bitcast(I32), 0)
 
+        tab_w0 = load_table(0)
         offs_t = load_list(offs, "offs_t")
         nc.sync.dma_start(w4_s[96:P, :].bitcast(I32), w4_scales.rearrange("a q n -> (a q) n").bitcast(I32))
-        tab_w0 = load_table(0)
-        raw00 = load_w1(held([P, PACK * 512], F32, "raw00")[:], 0, 0, 512)
+        raw_first = [load_w1(held([P, PACK * PAIR], F32, "raw_first%d" % a)[:], a, 0, PAIR) for a in range(2)]
         tab_w1 = load_table(1)
-        raw10 = [load_w1(held([P, PACK * 256], F32, "raw10_%d" % c0)[:], 1, c0, c0 + 256) for c0 in (0, 256)]
+        b1_c = load_plain(b1, "b1_plain")
         pos1_t = load_list(pos1, "pos1_t")
         pos2_t = load_list(pos2, "pos2_t")
-        b1_t = load_vector(b1, "b1_t")
-        gv_t = load_vector(gv, "gv_t")
+        raw_second = [
+            load_w1(held([P, PACK * PAIR], F32, "raw_second0")[:], 0, PAIR, KP),
+            load_w1(hz[:, SLOT : SLOT + S], 1, PAIR, KP),
+        ]
+        gv_c = load_plain(gv, "gv_plain")
+        raw_dealt = [
+            load_w1(hz[:, SLOT + S : 3 * SLOT], 0, KP, H),
+            load_w1(hz[:, 3 * SLOT : 3 * SLOT + PACK * KP], 1, KP, H),
+        ]
+        b1_c = b1_c + load_dealt(b1, "b1_dealt")
+        gv_c = gv_c + load_dealt(gv, "gv_dealt")
         w4_w = held([P, 2 * H], U16, "w4_w")
         nc.sync.dma_start(
             w4_w[:].bitcast(I32).rearrange("p (a n) -> p a n", a=2),
             w4_words.bitcast(I32).rearrange("a p n -> p a n"),
         )
-        raw01 = load_w1(hz[:, SLOT + S : 3 * SLOT], 0, 512, 1024)
-        raw11 = load_w1(hz[:, 3 * SLOT : 3 * SLOT + PACK * 512], 1, 512, 1024)
-        sc_t = load_vector(sc, "sc_t")
-        b2_t = load_vector(b2, "b2_t")
+        sc_c = load_plain(sc, "sc_plain") + load_dealt(sc, "sc_dealt")
+        b2_c = load_plain(b2, "b2_plain") + load_dealt(b2, "b2_dealt")
         pos3_t = load_list(pos3, "pos3_t")
 
         v_w = [held([P, S], U32, "v_w0")]
         v_s = held([P, S], U8, "v_s")
-        w1_w = [[held([P, KP], U32, "w1_w%d%d" % (a, b)) for b in range(2)] for a in range(2)]
-        w1_s = [[held([P, KP], U8, "w1_s%d%d" % (a, b)) for b in range(2)] for a in range(2)]
 
-        def gather_table(words, a):
-            for s in range(2):
+        def gather_table(words, a, step):
+            for j in range(0, S, step):
                 nc.vector.tensor_copy(
-                    v_w[a][:, s * BANK : (s + 1) * BANK], words[:].indirect(offs_t[:, s * 32 : (s + 1) * 32])
+                    v_w[a][:, j : j + step], words[:].indirect(offs_t[:, j // 16 : (j + step) // 16])
                 )
 
-        def deal_views(grouped, raw, m0):
-            width = raw.shape[2] // PACK
-            dst = grouped[:].rearrange("p (t m j) -> p m j t", t=PACK, j=PACK)[:, m0 : m0 + width]
-            return dst, raw.rearrange("p j (m t) -> p m j t", t=PACK)
+        def cast_plain(grouped, raw):
+            nc.scalar.activation(
+                grouped.rearrange("p (c i j) -> p c j i", i=4, j=PACK),
+                raw.rearrange("p j (c i) -> p c j i", i=4),
+                ACT.Copy,
+            )
 
-        def cast_w1(grouped, raw, m0=0):
-            dst, src = deal_views(grouped, raw, m0)
-            nc.scalar.activation(dst, src, ACT.Copy)
+        def cast_dealt(grouped, raw):
+            dst = grouped.rearrange("p (t m j) -> p m j t", t=PACK, j=PACK)
+            nc.scalar.activation(dst, raw.rearrange("p j (m t) -> p m j t", t=PACK), ACT.Copy)
 
         def quantise(words, scales, grouped, c0, c1):
             nc.vector.quantize_mx(
                 out=words[:, c0:c1].bitcast(E4M3), scales=scales[:, c0:c1], in_=grouped[:, PACK * c0 : PACK * c1]
             )
 
+        w1_q = {}
+
         def h_pass(bank, a, c, s):
-            b, t = divmod(c, PACK)
-            cols = slice(t * P, (t + 1) * P)
+            words, scales = w1_q[a, c]
             picks = slice(s * BANK, (s + 1) * BANK)
             nc.tensor.matmul_mx(
                 out=bank[:],
-                lhsT=w1_w[a][b][:, cols].bitcast(E4M3),
-                lhsT_scale=w1_s[a][b][:, cols],
+                lhsT=words.bitcast(E4M3),
+                lhsT_scale=scales,
                 rhs=v_w[a][:, picks].bitcast(E4M3),
                 rhs_scale=v_s[4 * a : P, picks],
                 start=(a == 0),
                 stop=(a == 1),
             )
 
-        z_planes = hz[:].rearrange("p (s x) -> p s x", x=SLOT)
-
         def h_rows(c, width=S):
             return hz[:, c * SLOT : c * SLOT + width]
 
+        def z_rows(c):
+            return hz[:, (c + 1) * SLOT + S : (c + 2) * SLOT]
+
+        def make_h(c):
+            banks = [psum.tile([P, BANK], F32, name="h_bank", tag="bank") for s in range(2)]
+            for a in range(2):
+                for s in range(2):
+                    h_pass(banks[s], a, c, s)
+            return banks
+
         def empty_h(banks, c):
             for s in range(2):
-                nc.scalar.activation(
-                    h_rows(c)[:, s * BANK : (s + 1) * BANK], banks[s][:], ACT.Identity, bias=b1_t[:, c : c + 1]
-                )
+                dst = h_rows(c)[:, s * BANK : (s + 1) * BANK]
+                if c == 0:
+                    nc.vector.tensor_scalar(dst, banks[s][:], b1_c[c], None, ALU.add)
+                else:
+                    nc.scalar.activation(dst, banks[s][:], ACT.Identity, bias=b1_c[c])
 
-        def new_banks(c):
-            return [psum.tile([P, BANK], F32, name="h_bank%d_%d" % (c, s), tag="bank") for s in range(2)]
+        def pair_tiles(name, first):
+            grouped = held([P, 2 * PACK * PAIR], BF16, name + "_g")
+            words = held([P, 2 * PAIR], U32, name + "_w")
+            scales = held([P, 2 * PAIR], U8, name + "_s")
+            for a in range(2):
+                for e in range(2):
+                    cols = slice(a * PAIR + e * P, a * PAIR + (e + 1) * P)
+                    w1_q[a, first + e] = words[:, cols], scales[:, cols]
+            return words, scales, grouped
 
         w4_rows = held([P, H], U8, "w4_rows")
+        nc.vector.tensor_copy(w4_rows[:, 0:KP], w4_s[:, 0:KP])
         nc.vector.tensor_copy(
-            w4_rows[:].rearrange("p (g t m) -> p g t m", t=PACK, m=P),
-            w4_s[:].rearrange("p (g m t) -> p g t m", t=PACK, m=P),
+            w4_rows[:, KP:H].rearrange("p (t m) -> p t m", t=PACK),
+            w4_s[:, KP:H].rearrange("p (m t) -> p t m", t=PACK),
         )
         for a in range(2):
             for q in range(4):
@@ -160,141 +191,146 @@ def tile_list_stopper_leak_features_kernel(
                 nc.sync.dma_start(
                     w4_sp[32 * q : 32 * q + 4, a * H : (a + 1) * H].bitcast(I32), w4_rows[row : row + 4, :].bitcast(I32)
                 )
-        gather_table(tab_w0, 0)
+        gather_table(tab_w0, 0, S)
         nc.vector.tensor_copy(v_s[:], tab_s[:].indirect(offs_t[:]))
         v_w.append(keep.tile([P, S], U32, name="v_w1", tag="tab_s", align_bytes=64))
-        g00 = held([P, PACK * KP], BF16, "g00")
-        cast_w1(g00, raw00)
-        quantise(w1_w[0][0], w1_s[0][0], g00, 0, KP)
-        gather_table(tab_w1, 1)
-        g10 = held([P, PACK * KP], BF16, "g10")
-        cast_w1(g10, raw10[0])
-        dst, src = deal_views(g10, raw10[1], 64)
-        nc.vector.tensor_copy(dst, src)
-        for t in range(PACK):
-            quantise(w1_w[1][0], w1_s[1][0], g10, t * P, (t + 1) * P)
-        w4_wp = held([P, 2 * H], U16, "w4_wp")
-        nc.vector.tensor_copy(
-            w4_wp[:].rearrange("p (g t m) -> p g t m", t=PACK, m=P),
-            w4_w[:].rearrange("p (g m t) -> p g t m", t=PACK, m=P),
-        )
+        first = pair_tiles("w1_first", 0)
+        for a in range(2):
+            cast_plain(first[2][:, a * PACK * PAIR : (a + 1) * PACK * PAIR], raw_first[a])
+            quantise(*first, a * PAIR, (a + 1) * PAIR)
+        gather_table(tab_w1, 1, BANK)
 
-        banks = [new_banks(c) for c in range(PACK)]
-        for c in range(PACK):
-            for a in range(2):
-                for s in range(2):
-                    h_pass(banks[c][s], a, c, s)
+        banks = [make_h(c) for c in range(2)]
+        second = pair_tiles("w1_second", 2)
+        empty_h(banks[0], 0)
+        for a in range(2):
+            cast_plain(second[2][:, a * PACK * PAIR : (a + 1) * PACK * PAIR], raw_second[a])
+        empty_h(banks[1], 1)
 
-        g01 = held([P, PACK * KP], BF16, "g01")
-        g11 = held([P, PACK * KP], BF16, "g11")
-        for c in range(2):
-            empty_h(banks[c], c)
-        cast_w1(g01, raw01)
-        empty_h(banks[2], 2)
-        cast_w1(g11, raw11)
-        empty_h(banks[3], 3)
-
-        def pick(c, m0, m1, width):
-            top = ring.tile([P, m1 - m0], F32, name="top", tag="top")
+        def pick(c, m0, m1, width, top=None):
+            if top is None:
+                top = ring.tile([P, m1 - m0], F32, name="top", tag="top")
             bottom = ring.tile([P, m1 - m0], F32, name="bottom", tag="bottom")
             cols = slice(m0 // 16, m1 // 16)
             nc.vector.tensor_copy(top[:], h_rows(c, width).indirect(pos1_t[:, cols]))
             nc.vector.tensor_copy(bottom[:], h_rows(c).indirect(pos2_t[:, cols]))
             return c, m0, m1, top, bottom
 
+        z_moved = held([P, PACK, M], F32, "z_moved")
+
         def join(c, m0, m1, top, bottom):
             nc.vector.scalar_tensor_tensor(
-                out=hz[:, (c + 1) * SLOT + S + m0 : (c + 1) * SLOT + S + m1],
-                in0=bottom[:],
-                scalar=gv_t[:, c : c + 1],
-                in1=top[:],
-                op0=ALU.mult,
-                op1=ALU.max,
+                out=z_rows(c)[:, m0:m1], in0=bottom[:], scalar=gv_c[c], in1=top[:], op0=ALU.mult, op1=ALU.max
             )
+            if c < PACK:
+                for t in range(PACK):
+                    nc.sync.dma_start(z_moved[32 * c : 32 * c + 32, t, :], z_rows(c)[t:P:PACK, :])
 
-        z_g = [held([P, PACK * M], BF16, "z_g%d" % b) for b in range(2)]
-        z_w = [held([P, M], U32, "z_w%d" % b) for b in range(2)]
-        z_s = [held([P, M], U8, "z_s%d" % b) for b in range(2)]
+        z_g = [held([P, PACK * M], BF16, "z_g%d" % a) for a in range(2)]
+        z_w = [held([P, M], U32, "z_w%d" % a) for a in range(2)]
+        z_s = [held([P, M], U8, "z_s%d" % a) for a in range(2)]
+        z_planes = [z_moved[:], hz[:].rearrange("p (s x) -> p s x", x=SLOT)[:, PACK + 1 :, S:]]
 
-        def weave(b, m0, m1):
-            planes = z_planes[:, PACK * b + 1 : PACK * b + 1 + PACK, S + m0 : S + m1]
-            nc.scalar.copy(
-                z_g[b][:, PACK * m0 : PACK * m1].rearrange("p (c i t) -> p c t i", i=4, t=PACK),
-                planes.rearrange("p t (c i) -> p c t i", i=4),
+        def weave(copy, a, m0, m1):
+            copy(
+                z_g[a][:, PACK * m0 : PACK * m1].rearrange("p (c i t) -> p c t i", i=4, t=PACK),
+                z_planes[a][:, :, m0:m1].rearrange("p t (c i) -> p c t i", i=4),
             )
 
         scaled = {}
-        out_order = [(c + PACK) % TILES for c in range(TILES)]
+
+        def scaled_slot(shape, dtype, name):
+            return ring.tile(shape, dtype, name=name, tag="scaled", bufs=SC_AHEAD, align_bytes=64)
 
         def scale_h(c):
-            scaled[c] = ring.tile([P, S], F32, name="scaled", tag="scaled")
-            nc.scalar.activation(scaled[c][:], h_rows(c), ACT.Copy, scale=sc_t[:, c : c + 1])
+            scaled[c] = scaled_slot([P, S], F32, "scaled")
+            nc.scalar.activation(scaled[c][:], h_rows(c), ACT.Copy, scale=sc_c[c])
+
+        dealt = []
+        for a, make in enumerate((held, scaled_slot)):
+            words = make([P, KP], U32, "w1_dealt_w%d" % a)
+            scales = make([P, KP], U8, "w1_dealt_s%d" % a)
+            dealt.append((words, scales, held([P, PACK * KP], BF16, "w1_dealt_g%d" % a)))
+            for t in range(PACK):
+                w1_q[a, PACK + t] = words[:, t * P : (t + 1) * P], scales[:, t * P : (t + 1) * P]
 
         picked = pick(0, 0, M, S)
+        quantise(*second, 0, 2 * PAIR)
+        banks = [make_h(c) for c in (2, 3)]
+        for a in range(2):
+            cast_dealt(dealt[a][2][:], raw_dealt[a])
+            empty_h(banks[a], 2 + a)
         for c in range(1, PACK):
             ahead = pick(c, 0, M, SLOT)
             join(*picked)
             picked = ahead
-            if c == 1:
-                quantise(w1_w[0][1], w1_s[0][1], g01, 0, KP)
-            if c == 2:
-                quantise(w1_w[1][1], w1_s[1][1], g11, 0, KP)
+            if c < 3:
+                quantise(*dealt[c - 1], 0, KP)
         for c in range(PACK, TILES):
-            banks = new_banks(c)
-            for a in range(2):
-                for s in range(2):
-                    h_pass(banks[s], a, c, s)
-            empty_h(banks, c)
+            empty_h(make_h(c), c)
         for c in range(PACK, TILES - 1):
             ahead = pick(c, 0, M, SLOT)
             join(*picked)
             picked = ahead
             if c == PACK:
-                weave(0, 0, M)
-                for first in out_order[:SC_AHEAD]:
-                    scale_h(first)
+                weave(nc.scalar.copy, 0, 0, M)
+                for early in range(SC_AHEAD):
+                    scale_h(early)
         quantise(z_w[0], z_s[0], z_g[0], 0, M)
         for m0, m1 in LAST_Z:
-            ahead = pick(TILES - 1, m0, m1, SLOT if m0 == 0 else S)
+            if m0 == 0:
+                ahead = pick(TILES - 1, m0, m1, SLOT, held([P, m1], F32, "z_g0"))
+            else:
+                ahead = pick(TILES - 1, m0, m1, S)
             join(*picked)
             picked = ahead
         join(*picked)
         for m0, m1 in LAST_Z:
-            weave(1, m0, m1)
+            weave(nc.vector.tensor_copy if m1 == M else nc.scalar.copy, 1, m0, m1)
             quantise(z_w[1], z_s[1], z_g[1], m0, m1)
+        w4_dealt = keep.tile([P, 2 * KP], U16, name="w4_dealt", tag="z_g1", align_bytes=64)
+        nc.vector.tensor_copy(
+            w4_dealt[:].rearrange("p (a t m) -> p a t m", a=2, t=PACK),
+            w4_w[:].rearrange("p (a b m t) -> p a b t m", a=2, b=2, t=PACK)[:, :, 1],
+        )
+
+        def w4_words_of(a, c):
+            if c < PACK:
+                return w4_w[:, a * H + c * P : a * H + (c + 1) * P]
+            return w4_dealt[:, a * KP + (c - PACK) * P : a * KP + (c - PACK + 1) * P]
 
         def y_group(c, m0, m1, step, squares):
             bank = psum.tile([P, m1 - m0], F32, name="y_bank", tag="bank")
             for a in range(2):
-                cols = slice(a * H + c * P, a * H + (c + 1) * P)
                 for m in range(m0, m1, step):
                     nc.tensor.matmul_mx(
                         out=bank[:, m - m0 : m - m0 + step],
-                        lhsT=w4_wp[:, cols].bitcast(E2M1),
-                        lhsT_scale=w4_sp[:, cols],
+                        lhsT=w4_words_of(a, c).bitcast(E2M1),
+                        lhsT_scale=w4_sp[:, a * H + c * P : a * H + (c + 1) * P],
                         rhs=z_w[a][:, m : m + step].bitcast(E4M3),
                         rhs_scale=z_s[a][:, m : m + step],
                         start=(a == 0 and m == m0),
                         stop=(a == 1 and m + step == m1),
                     )
-            nc.scalar.activation(squares[:, m0:m1], bank[:], ACT.Square, bias=b2_t[:, c : c + 1])
+            nc.scalar.activation(squares[:, m0:m1], bank[:], ACT.Square, bias=b2_c[c])
 
-        out_rows = out.rearrange("(b p t) j -> b t p j", p=P, t=PACK)
-        for i, c in enumerate(out_order):
+        out_dealt = out[KP:H, :].rearrange("(p t) j -> t p j", t=PACK)
+        for c in range(TILES):
             squares = ring.tile([P, Y_WIN], F32, name="squares", tag="squares")
-            if i == 0:
+            if c == 0:
                 y_group(c, 0, M - P, P, squares)
                 y_group(c, M - P, M, P, squares)
             else:
                 y_group(c, 0, M, M, squares)
-            if i >= SC_AHEAD:
+            if c >= SC_AHEAD:
                 scale_h(c)
             result = ring.tile([P, S], F32, name="result", tag="result", bufs=4)
-            for j0, j1 in LAST_OUT if i == TILES - 1 else [(0, S)]:
+            rows = out[c * P : (c + 1) * P, :] if c < PACK else out_dealt[c - PACK]
+            for j0, j1 in LAST_OUT if c == TILES - 1 else [(0, S)]:
                 nc.vector.tensor_tensor(
                     result[:, j0:j1],
                     squares[:].indirect(pos3_t[:, j0 // 16 : j1 // 16]),
                     scaled[c][:, j0:j1],
                     ALU.add,
                 )
-                nc.sync.dma_start(out_rows[c // PACK, c % PACK, :, j0:j1], result[:, j0:j1])
+                nc.sync.dma_start(rows[:, j0:j1], result[:, j0:j1])

from contextlib import ExitStack

import concourse.mybir as mybir

K, H, T, S, M = 1024, 1024, 4096, 1024, 512
FLOPS = 2 * K * H * S + 2 * H * H * M

F32 = mybir.dt.float32
BF16 = mybir.dt.bfloat16
I32 = mybir.dt.int32
U32 = mybir.dt.uint32
U16 = mybir.dt.uint16
U8 = mybir.dt.uint8
E4M3 = mybir.dt.float8_e4m3fn_x4
E2M1 = mybir.dt.float4_e2m1fn_x4
ALU = mybir.AluOpType
ACT = mybir.ActivationFunctionType

P = 128
PACK = 4
KP = P * PACK
BANK = 512
TILES = H // P
PAIR = 2 * P
SLOT = S + M
Y_WIN = S + 32
SC_AHEAD = 2
LAST_Z = [(0, 256), (256, 384), (384, 512)]
LAST_OUT = [(0, 512), (512, 896), (896, 1024)]


def tile_list_stopper_leak_features_kernel(
    tc, tab_words, tab_scales, offs, pos1, pos2, pos3, w1, b1, gv, w4_words, w4_scales, b2, sc, out
):
    nc = tc.nc
    with ExitStack() as ctx:
        keep = ctx.enter_context(tc.tile_pool(name="keep", bufs=1))
        ring = ctx.enter_context(tc.tile_pool(name="ring", bufs=3))
        psum = ctx.enter_context(tc.psum_pool(name="psum", bufs=8))

        def held(shape, dtype, name):
            return keep.tile(shape, dtype, name=name, tag=name, align_bytes=64)

        def load_list(src, name):
            lst = keep.tile(list(src.shape), U16, name=name)
            nc.sync.dma_start(lst[:], src)
            return lst

        def load_table(a):
            words = held([P, T], U32, "tab_w%d" % a)
            nc.sync.dma_start(words[:].bitcast(I32), tab_words[a].rearrange("p t i -> p (t i)").bitcast(I32))
            return words

        hz = held([P, (TILES + 1) * SLOT], F32, "hz")

        def load_w1(raw, a, c0, c1):
            raw = raw.rearrange("p (j c) -> p j c", j=PACK)
            nc.sync.dma_start(raw, w1[a * KP : (a + 1) * KP, c0:c1].rearrange("(p j) c -> p j c", j=PACK))
            return raw

        def load_plain(src, name):
            vec = held([P, PACK], F32, name)
            with nc.allow_non_contiguous_dma(reason="one value a partition and tile"):
                nc.sync.dma_start(vec[:], src[0:KP].rearrange("(c p) -> p c", p=P))
            return [vec[:, c : c + 1] for c in range(PACK)]

        def load_dealt(src, name):
            vec = held([P, PACK], F32, name)
            nc.sync.dma_start(vec[:], src[KP:H].rearrange("(p t) -> p t", t=PACK))
            return [vec[:, t : t + 1] for t in range(PACK)]

        tab_s = keep.tile([P, T], U8, name="tab_s", tag="tab_s", align_bytes=64)
        nc.vector.memset(tab_s[:].bitcast(I32), 0)
        for q in range(4):
            nc.gpsimd.dma_start(
                tab_s[32 * q : 32 * q + 8, :].bitcast(I32), tab_scales[:, 4 * q : 4 * q + 4, :].bitcast(I32)
            )
        w4_s = held([P, H], U8, "w4_s")
        nc.vector.memset(w4_s[0:96, :].bitcast(I32), 0)
        w4_sp = held([P, 2 * H], U8, "w4_sp")
        nc.vector.memset(w4_sp[:].bitcast(I32), 0)

        tab_w0 = load_table(0)
        offs_t = load_list(offs, "offs_t")
        nc.sync.dma_start(w4_s[96:P, :].bitcast(I32), w4_scales.rearrange("a q n -> (a q) n").bitcast(I32))
        raw_first = [load_w1(held([P, PACK * PAIR], F32, "raw_first%d" % a)[:], a, 0, PAIR) for a in range(2)]
        tab_w1 = load_table(1)
        b1_c = load_plain(b1, "b1_plain")
        pos1_t = load_list(pos1, "pos1_t")
        pos2_t = load_list(pos2, "pos2_t")
        raw_second = [
            load_w1(held([P, PACK * PAIR], F32, "raw_second0")[:], 0, PAIR, KP),
            load_w1(hz[:, SLOT : SLOT + S], 1, PAIR, KP),
        ]
        gv_c = load_plain(gv, "gv_plain")
        raw_dealt = [
            load_w1(hz[:, SLOT + S : 3 * SLOT], 0, KP, H),
            load_w1(hz[:, 3 * SLOT : 3 * SLOT + PACK * KP], 1, KP, H),
        ]
        b1_c = b1_c + load_dealt(b1, "b1_dealt")
        gv_c = gv_c + load_dealt(gv, "gv_dealt")
        w4_w = held([P, 2 * H], U16, "w4_w")
        nc.sync.dma_start(
            w4_w[:].bitcast(I32).rearrange("p (a n) -> p a n", a=2),
            w4_words.bitcast(I32).rearrange("a p n -> p a n"),
        )
        sc_c = load_plain(sc, "sc_plain") + load_dealt(sc, "sc_dealt")
        b2_c = load_plain(b2, "b2_plain") + load_dealt(b2, "b2_dealt")
        pos3_t = load_list(pos3, "pos3_t")

        v_w = [held([P, S], U32, "v_w0")]
        v_s = held([P, S], U8, "v_s")

        def gather_table(words, a, step):
            for j in range(0, S, step):
                nc.vector.tensor_copy(
                    v_w[a][:, j : j + step], words[:].indirect(offs_t[:, j // 16 : (j + step) // 16])
                )

        def cast_plain(grouped, raw):
            nc.scalar.activation(
                grouped.rearrange("p (c i j) -> p c j i", i=4, j=PACK),
                raw.rearrange("p j (c i) -> p c j i", i=4),
                ACT.Copy,
            )

        def cast_dealt(grouped, raw):
            dst = grouped.rearrange("p (t m j) -> p m j t", t=PACK, j=PACK)
            nc.scalar.activation(dst, raw.rearrange("p j (m t) -> p m j t", t=PACK), ACT.Copy)

        def quantise(words, scales, grouped, c0, c1):
            nc.vector.quantize_mx(
                out=words[:, c0:c1].bitcast(E4M3), scales=scales[:, c0:c1], in_=grouped[:, PACK * c0 : PACK * c1]
            )

        w1_q = {}

        def h_pass(bank, a, c, s):
            words, scales = w1_q[a, c]
            picks = slice(s * BANK, (s + 1) * BANK)
            nc.tensor.matmul_mx(
                out=bank[:],
                lhsT=words.bitcast(E4M3),
                lhsT_scale=scales,
                rhs=v_w[a][:, picks].bitcast(E4M3),
                rhs_scale=v_s[4 * a : P, picks],
                start=(a == 0),
                stop=(a == 1),
            )

        def h_rows(c, width=S):
            return hz[:, c * SLOT : c * SLOT + width]

        def z_rows(c):
            return hz[:, (c + 1) * SLOT + S : (c + 2) * SLOT]

        def make_h(c):
            banks = [psum.tile([P, BANK], F32, name="h_bank", tag="bank") for s in range(2)]
            for a in range(2):
                for s in range(2):
                    h_pass(banks[s], a, c, s)
            return banks

        def empty_h(banks, c):
            for s in range(2):
                dst = h_rows(c)[:, s * BANK : (s + 1) * BANK]
                if c == 0:
                    nc.vector.tensor_scalar(dst, banks[s][:], b1_c[c], None, ALU.add)
                else:
                    nc.scalar.activation(dst, banks[s][:], ACT.Identity, bias=b1_c[c])

        def pair_tiles(name, first):
            grouped = held([P, 2 * PACK * PAIR], BF16, name + "_g")
            words = held([P, 2 * PAIR], U32, name + "_w")
            scales = held([P, 2 * PAIR], U8, name + "_s")
            for a in range(2):
                for e in range(2):
                    cols = slice(a * PAIR + e * P, a * PAIR + (e + 1) * P)
                    w1_q[a, first + e] = words[:, cols], scales[:, cols]
            return words, scales, grouped

        w4_rows = held([P, H], U8, "w4_rows")
        nc.vector.tensor_copy(w4_rows[:, 0:KP], w4_s[:, 0:KP])
        nc.vector.tensor_copy(
            w4_rows[:, KP:H].rearrange("p (t m) -> p t m", t=PACK),
            w4_s[:, KP:H].rearrange("p (m t) -> p t m", t=PACK),
        )
        for a in range(2):
            for q in range(4):
                row = 96 + 16 * a + 4 * q
                nc.sync.dma_start(
                    w4_sp[32 * q : 32 * q + 4, a * H : (a + 1) * H].bitcast(I32), w4_rows[row : row + 4, :].bitcast(I32)
                )
        gather_table(tab_w0, 0, S)
        nc.vector.tensor_copy(v_s[:], tab_s[:].indirect(offs_t[:]))
        v_w.append(keep.tile([P, S], U32, name="v_w1", tag="tab_s", align_bytes=64))
        first = pair_tiles("w1_first", 0)
        for a in range(2):
            cast_plain(first[2][:, a * PACK * PAIR : (a + 1) * PACK * PAIR], raw_first[a])
            quantise(*first, a * PAIR, (a + 1) * PAIR)
        gather_table(tab_w1, 1, BANK)

        banks = [make_h(c) for c in range(2)]
        second = pair_tiles("w1_second", 2)
        empty_h(banks[0], 0)
        for a in range(2):
            cast_plain(second[2][:, a * PACK * PAIR : (a + 1) * PACK * PAIR], raw_second[a])
        empty_h(banks[1], 1)

        def pick(c, m0, m1, width, top=None):
            if top is None:
                top = ring.tile([P, m1 - m0], F32, name="top", tag="top")
            bottom = ring.tile([P, m1 - m0], F32, name="bottom", tag="bottom")
            cols = slice(m0 // 16, m1 // 16)
            nc.vector.tensor_copy(top[:], h_rows(c, width).indirect(pos1_t[:, cols]))
            nc.vector.tensor_copy(bottom[:], h_rows(c).indirect(pos2_t[:, cols]))
            return c, m0, m1, top, bottom

        z_moved = held([P, PACK, M], F32, "z_moved")

        def join(c, m0, m1, top, bottom):
            nc.vector.scalar_tensor_tensor(
                out=z_rows(c)[:, m0:m1], in0=bottom[:], scalar=gv_c[c], in1=top[:], op0=ALU.mult, op1=ALU.max
            )
            if c < PACK:
                for t in range(PACK):
                    nc.sync.dma_start(z_moved[32 * c : 32 * c + 32, t, :], z_rows(c)[t:P:PACK, :])

        z_g = [held([P, PACK * M], BF16, "z_g%d" % a) for a in range(2)]
        z_w = [held([P, M], U32, "z_w%d" % a) for a in range(2)]
        z_s = [held([P, M], U8, "z_s%d" % a) for a in range(2)]
        z_planes = [z_moved[:], hz[:].rearrange("p (s x) -> p s x", x=SLOT)[:, PACK + 1 :, S:]]

        def weave(copy, a, m0, m1):
            copy(
                z_g[a][:, PACK * m0 : PACK * m1].rearrange("p (c i t) -> p c t i", i=4, t=PACK),
                z_planes[a][:, :, m0:m1].rearrange("p t (c i) -> p c t i", i=4),
            )

        scaled = {}

        def scaled_slot(shape, dtype, name):
            return ring.tile(shape, dtype, name=name, tag="scaled", bufs=SC_AHEAD, align_bytes=64)

        def scale_h(c):
            scaled[c] = scaled_slot([P, S], F32, "scaled")
            nc.scalar.activation(scaled[c][:], h_rows(c), ACT.Copy, scale=sc_c[c])

        dealt = []
        for a, make in enumerate((held, scaled_slot)):
            words = make([P, KP], U32, "w1_dealt_w%d" % a)
            scales = make([P, KP], U8, "w1_dealt_s%d" % a)
            dealt.append((words, scales, held([P, PACK * KP], BF16, "w1_dealt_g%d" % a)))
            for t in range(PACK):
                w1_q[a, PACK + t] = words[:, t * P : (t + 1) * P], scales[:, t * P : (t + 1) * P]

        picked = pick(0, 0, M, S)
        quantise(*second, 0, 2 * PAIR)
        banks = [make_h(c) for c in (2, 3)]
        for a in range(2):
            cast_dealt(dealt[a][2][:], raw_dealt[a])
            empty_h(banks[a], 2 + a)
        for c in range(1, PACK):
            ahead = pick(c, 0, M, SLOT)
            join(*picked)
            picked = ahead
            if c < 3:
                quantise(*dealt[c - 1], 0, KP)
        for c in range(PACK, TILES):
            empty_h(make_h(c), c)
        for c in range(PACK, TILES - 1):
            ahead = pick(c, 0, M, SLOT)
            join(*picked)
            picked = ahead
            if c == PACK:
                weave(nc.scalar.copy, 0, 0, M)
                for early in range(SC_AHEAD):
                    scale_h(early)
        quantise(z_w[0], z_s[0], z_g[0], 0, M)
        for m0, m1 in LAST_Z:
            if m0 == 0:
                ahead = pick(TILES - 1, m0, m1, SLOT, held([P, m1], F32, "z_g0"))
            else:
                ahead = pick(TILES - 1, m0, m1, S)
            join(*picked)
            picked = ahead
        join(*picked)
        for m0, m1 in LAST_Z:
            weave(nc.vector.tensor_copy if m1 == M else nc.scalar.copy, 1, m0, m1)
            quantise(z_w[1], z_s[1], z_g[1], m0, m1)
        w4_dealt = keep.tile([P, 2 * KP], U16, name="w4_dealt", tag="z_g1", align_bytes=64)
        nc.vector.tensor_copy(
            w4_dealt[:].rearrange("p (a t m) -> p a t m", a=2, t=PACK),
            w4_w[:].rearrange("p (a b m t) -> p a b t m", a=2, b=2, t=PACK)[:, :, 1],
        )

        def w4_words_of(a, c):
            if c < PACK:
                return w4_w[:, a * H + c * P : a * H + (c + 1) * P]
            return w4_dealt[:, a * KP + (c - PACK) * P : a * KP + (c - PACK + 1) * P]

        def y_group(c, m0, m1, step, squares):
            bank = psum.tile([P, m1 - m0], F32, name="y_bank", tag="bank")
            for a in range(2):
                for m in range(m0, m1, step):
                    nc.tensor.matmul_mx(
                        out=bank[:, m - m0 : m - m0 + step],
                        lhsT=w4_words_of(a, c).bitcast(E2M1),
                        lhsT_scale=w4_sp[:, a * H + c * P : a * H + (c + 1) * P],
                        rhs=z_w[a][:, m : m + step].bitcast(E4M3),
                        rhs_scale=z_s[a][:, m : m + step],
                        start=(a == 0 and m == m0),
                        stop=(a == 1 and m + step == m1),
                    )
            nc.scalar.activation(squares[:, m0:m1], bank[:], ACT.Square, bias=b2_c[c])

        out_dealt = out[KP:H, :].rearrange("(p t) j -> t p j", t=PACK)
        for c in range(TILES):
            squares = ring.tile([P, Y_WIN], F32, name="squares", tag="squares")
            if c == 0:
                y_group(c, 0, M - P, P, squares)
                y_group(c, M - P, M, P, squares)
            else:
                y_group(c, 0, M, M, squares)
            if c >= SC_AHEAD:
                scale_h(c)
            result = ring.tile([P, S], F32, name="result", tag="result", bufs=4)
            rows = out[c * P : (c + 1) * P, :] if c < PACK else out_dealt[c - PACK]
            for j0, j1 in LAST_OUT if c == TILES - 1 else [(0, S)]:
                nc.vector.tensor_tensor(
                    result[:, j0:j1],
                    squares[:].indirect(pos3_t[:, j0 // 16 : j1 // 16]),
                    scaled[c][:, j0:j1],
                    ALU.add,
                )
                nc.sync.dma_start(rows[:, j0:j1], result[:, j0:j1])
